import numpy as np, ml_dtypes
CORES = [5,29,101,125,133,157,229,253]
N = 8
R, TK = 16, 512
def setup_inputs(rng):
    u = (rng.standard_normal((N, 128, R), dtype=np.float32) / 11).astype(ml_dtypes.bfloat16)
    return {"x": rng.standard_normal((N, 128, TK), dtype=np.float32).astype(ml_dtypes.bfloat16), "u": u, "ut": u.transpose(0, 2, 1).copy(), "vt": rng.standard_normal((N, R, 128), dtype=np.float32).astype(ml_dtypes.bfloat16)}
def setup_inputs_big(rng):
    d = setup_inputs(rng)
    for k in ("x", "u", "ut", "vt"): d[k] = (d[k].astype(np.float32) * 1024.0).astype(d[k].dtype)
    return d
def setup_inputs_small(rng):
    d = setup_inputs(rng)
    for k in ("x", "u", "ut", "vt"): d[k] = (d[k].astype(np.float32) * (1 / 1024.0)).astype(d[k].dtype)
    return d
def setup_inputs_apart(rng):
    d = setup_inputs(rng)
    f = (10.0 ** rng.permutation(np.linspace(-1.5, 1.5, N))).astype(np.float32).reshape(N, 1, 1)
    for k in ("x", "u", "ut", "vt"): d[k] = (d[k].astype(np.float32) * f).astype(d[k].dtype)
    return d
def tie_inputs(x):
    x = dict(x)
    x["ut"] = x["u"].transpose(0, 2, 1).copy()
    return x
def reference(x, u, ut, vt):
    X, U, VT = x.astype(np.float64), u.astype(np.float64), vt.astype(np.float64)
    y = np.stack([sum(VT[j].T @ (U[j].T @ X[r]) for j in range(N)) for r in range(N)])
    return {"y": y.astype(ml_dtypes.bfloat16 if x.dtype != np.float64 else np.float64)}

from concourse.bass import DstId, RemoteDMATransfer

R = 16
HELPERS = 2
E_HOP1 = 2
E_HOP2 = 2
E_PLANE = 1
BLK = 256

SCRATCH = {
    "G": ("dram", [8, 128, 32], "bfloat16"),
    "X": ("sbuf", [128, 512], "bfloat16"),
    "FU": ("sbuf", [128, 128], "bfloat16"),
    "FV": ("sbuf", [128, 128], "bfloat16"),
    "Wb": ("sbuf", [128, 128], "bfloat16"),
    "Yb": ("sbuf", [128, 512], "bfloat16"),
    "Wp": ("psum", [128, 512], "float32"),
    "Yp0": ("psum", [128, 512], "float32"),
    "Yp1": ("psum", [128, 512], "float32"),
}
SEMAPHORES = ["staged", "sent1", "sent2", "arrH", "arrS", "arrC", "xl", "ready", "wm", "wc",
              "ym0", "ym1", "yc0", "yc1", "stored"]


def _engines(m):
    return [e for e in range(m.bit_length()) if (m >> e) & 1]


def _mask(es):
    m = 0
    for e in es:
        m |= 1 << e
    return m


def _plan(T, topo):
    cores = list(T.cores)
    first = cores[0]
    near = [c for c in cores if c == first or topo.same_plane(first, c)]
    far = [c for c in cores if c not in near]
    slot = {c: i for i, c in enumerate(near + far)}
    world = (max(topo.host(c) for c in cores) + 1) * topo.CORES_PER_HOST
    info = {}
    for c in cores:
        mine, other = (near, far) if c in near else (far, near)
        helpers = [w for w in range(world)
                   if topo.host(w) == topo.host(c) and topo.chip(w) == topo.chip(c) and topo.die(w) == topo.die(c)
                   and w not in cores and all(topo.may_write(w, d) for d in other)][:HELPERS]
        info[c] = (mine, other, helpers)
    return slot, info


def _send(g, topo, core, dsts, engine_sets, ap, remote_sem, local_sem):
    trs = []
    for d, es in zip(dsts, engine_sets):
        rid, pid = topo.addr(d, core)
        trs.append(RemoteDMATransfer(dst_ids=[DstId(rid=rid, pnc=pid)], dma_engine_mask=_mask(es),
                                     remote_sem=remote_sem, src=ap, dst=ap))
    g.remote_dma_fused(trs, local_sem=local_sem)


def _spread(es, n, k):
    o = es[0::2] + es[1::2]
    return [o[i * k:(i + 1) * k] for i in range(n)]


def rank_program(g, core, T, topo):
    slot, info = _plan(T, topo)
    s = T.sem
    rank = T.rank_of(core)

    if rank is None:
        for c in T.cores:
            mine, other, helpers = info[c]
            if core in helpers:
                h = helpers.index(core)
                n = len(other) // len(helpers)
                dsts = other[h * n:(h + 1) * n]
                g.wait_ge(s.arrH, E_HOP1)
                _send(g, topo, core, dsts, _spread(_engines(topo.mask(core, dsts[0])), n, E_HOP2),
                      T.G[slot[c]], s.arrC, s.sent1)
                g.wait_ge(s.sent1, n * E_HOP2)
        return

    mine, other, helpers = info[core]
    p = slot[core]
    peers = [d for d in mine if d != core]
    lo, clo, ng = slot[mine[0]], slot[other[0]], len(mine)

    g.sync.dma_start(T.G[p, 0:64, :], T.ut[:, :]).then_inc(s.staged, 16)
    g.scalar.dma_start(T.G[p, 64:128, :], T.vt[:, :]).then_inc(s.staged, 16)

    off = _engines(topo.mask(core, peers[0]))
    on = [e for e in _engines(topo.mask(core, helpers[0])) if e not in off]
    g.wait_ge(s.staged, 32)
    _send(g, topo, core, helpers, _spread(on, len(helpers), E_HOP1), T.G[p], s.arrH, s.sent1)
    _send(g, topo, core, peers, _spread(off, len(peers), E_PLANE), T.G[p], s.arrS, s.sent2)

    g.sync.wait_ge(s.sent1, len(helpers) * E_HOP1)
    g.sync.dma_start(T.X[:, :], T.x[:, :]).then_inc(s.xl, 16)

    for q, F, a, b in ((g.sync, T.FU, 0, 64), (g.scalar, T.FV, 64, 128)):
        q.wait_ge(s.staged, 32)
        q.wait_ge(s.arrS, len(peers) * E_PLANE)
        q.dma_start(F[lo * R:(lo + ng) * R, :], T.G[lo:lo + ng, a:b, :]).then_inc(s.ready, 16)
        q.wait_ge(s.arrC, len(other) * E_HOP2)
        q.dma_start(F[clo * R:(clo + ng) * R, :], T.G[clo:clo + ng, a:b, :]).then_inc(s.ready, 16)

    g.tensor.wait_ge(s.ready, 64)
    g.tensor.matmul(T.Wp[:, 0:128], T.FU[:, :], T.FV[:, :], True, True).then_inc(s.wm, 1)
    g.vector.wait_ge(s.wm, 1)
    g.vector.tensor_copy(T.Wb[:, :], T.Wp[:, 0:128]).then_inc(s.wc, 1)
    g.tensor.wait_ge(s.xl, 16)
    g.tensor.wait_ge(s.wc, 1)
    blocks = ((T.Yp0, s.ym0, s.yc0, g.sync), (T.Yp1, s.ym1, s.yc1, g.scalar))
    for i, (Yp, ym, yc, q) in enumerate(blocks):
        g.tensor.matmul(Yp[:, 0:BLK], T.Wb[:, :], T.X[:, i * BLK:(i + 1) * BLK], True, True).then_inc(ym, 1)
    for i, (Yp, ym, yc, q) in enumerate(blocks):
        g.vector.wait_ge(ym, 1)
        g.vector.tensor_copy(T.Yb[:, i * BLK:(i + 1) * BLK], Yp[:, 0:BLK]).then_inc(yc, 1)
        q.wait_ge(yc, 1)
        q.dma_start(T.y[:, i * BLK:(i + 1) * BLK], T.Yb[:, i * BLK:(i + 1) * BLK]).then_inc(s.stored, 16)

    g.wait_ge(s.sent2, len(peers) * E_PLANE)
    g.wait_ge(s.stored, 32)
